import numpy as np, ml_dtypes
CORES = [65,73,81,89,97,105,113,121]
N = 8
R, TK = 8, 512
def setup_inputs(rng):
    u = (rng.standard_normal((N, 128, R), dtype=np.float32) / 11).astype(ml_dtypes.bfloat16)
    return {"x": rng.standard_normal((N, 128, TK), dtype=np.float32).astype(ml_dtypes.bfloat16), "u": u, "ut": u.transpose(0, 2, 1).copy(), "vt": rng.standard_normal((N, R, 128), dtype=np.float32).astype(ml_dtypes.bfloat16)}
def setup_inputs_big(rng):
    d = setup_inputs(rng)
    for k in ("x", "u", "ut", "vt"): d[k] = (d[k].astype(np.float32) * 1024.0).astype(d[k].dtype)
    return d
def setup_inputs_small(rng):
    d = setup_inputs(rng)
    for k in ("x", "u", "ut", "vt"): d[k] = (d[k].astype(np.float32) * (1 / 1024.0)).astype(d[k].dtype)
    return d
def setup_inputs_apart(rng):
    d = setup_inputs(rng)
    f = (10.0 ** rng.permutation(np.linspace(-1.5, 1.5, N))).astype(np.float32).reshape(N, 1, 1)
    for k in ("x", "u", "ut", "vt"): d[k] = (d[k].astype(np.float32) * f).astype(d[k].dtype)
    return d
def tie_inputs(x):
    x = dict(x)
    x["ut"] = x["u"].transpose(0, 2, 1).copy()
    return x
def reference(x, u, ut, vt):
    X, U, VT = x.astype(np.float64), u.astype(np.float64), vt.astype(np.float64)
    y = np.stack([sum(VT[j].T @ (U[j].T @ X[r]) for j in range(N)) for r in range(N)])
    return {"y": y.astype(ml_dtypes.bfloat16 if x.dtype != np.float64 else np.float64)}

from concourse.bass import DstId, RemoteDMATransfer

N, R, D, TK = 8, 8, 128, 512
HALF = TK // 2

SCRATCH = {
    "gat": ("dram", [N, 128, 2 * R * D // 128], "bfloat16"),
    "uv": ("sbuf", [128, 2 * D], "bfloat16"),
    "xs": ("sbuf", [128, TK], "bfloat16"),
    "wb": ("sbuf", [128, D], "bfloat16"),
    "ys": ("sbuf", [128, TK], "bfloat16"),
    "wp": ("psum", [128, 512], "float32"),
    "yp0": ("psum", [128, 512], "float32"),
    "yp1": ("psum", [128, 512], "float32"),
}
SEMAPHORES = ["ld", "xl", "hop", "near", "far", "sent", "gnear", "gfar", "mw", "cw", "my0", "my1", "cy0", "cy1", "st"]


def _planes(T, topo):
    cores = list(T.cores)
    first = topo.chip(cores[0])
    planes = [[], []]
    for c in cores:
        ch = topo.chip(c)
        planes[0 if (ch == first or topo.same_plane(ch, first)) else 1].append(c)
    slot = {}
    for c in planes[0] + planes[1]:
        slot[c] = len(slot)
    return planes, slot


def _routes(c, planes, T, topo):
    mine, other = (planes[0], planes[1]) if c in planes[0] else (planes[1], planes[0])
    i = mine.index(c)
    near = mine[i + 1:] + mine[:i]
    turn = other[i + 1:] + other[:i + 1]
    far = [d for d in turn if not topo.mates(topo.chip(c), topo.chip(d))]
    far += [d for d in turn if topo.mates(topo.chip(c), topo.chip(d))]
    helpers = [h for h in range(topo.CHIPS * topo.CORES_PER_CHIP)
               if T.rank_of(h) is None and topo.chip(h) == topo.chip(c) and topo.die(h) == topo.die(c)
               and all(topo.may_write(h, d) for d in far)]
    share = {}
    for k, h in enumerate(helpers):
        share[h] = far[k::len(helpers)]
    return near, share


def _engine(src, dsts, topo):
    m = topo.mask(src, dsts[0])
    for d in dsts:
        m &= topo.mask(src, d)
    return m & -m


def _send(g, T, topo, dsts, s, engine, sem):
    ids = []
    for d in dsts:
        a = topo.addr(d)
        ids.append(DstId(rid=a[0], pnc=a[1]))
    g.remote_dma_fused(
        [RemoteDMATransfer(dst_ids=ids, dma_engine_mask=engine, remote_sem=sem,
                           srcs=[T.gat[s]], dsts=[T.gat[s] for d in dsts], alu_op=0)],
        local_sem=T.sem.sent)


def rank_program(g, core, T, topo):
    S = T.sem
    planes, slot = _planes(T, topo)

    if T.rank_of(core) is None:
        for c in T.cores:
            if topo.chip(c) != topo.chip(core):
                continue
            share = _routes(c, planes, T, topo)[1]
            if core in share:
                g.wait_ge(S.hop, 1)
                _send(g, T, topo, share[core], slot[c], _engine(core, share[core], topo), S.far)
                g.wait_ge(S.sent, 1)
        return

    near, share = _routes(core, planes, T, topo)
    helpers = list(share)
    s = slot[core]
    mine, other = (planes[0], planes[1]) if core in planes[0] else (planes[1], planes[0])
    a0, a1 = slot[mine[0]], slot[mine[0]] + len(mine)
    b0, b1 = slot[other[0]], slot[other[0]] + len(other)
    hr = R * D // 16

    g.sync.dma_start(T.gat[s, 0:hr, :], T.ut[:, :]).then_inc(S.ld, 16)
    g.scalar.dma_start(T.gat[s, hr:2 * hr, :], T.vt[:, :]).then_inc(S.ld, 16)
    g.sync.dma_start(T.xs[:, :], T.x[:, :]).then_inc(S.xl, 16)

    eng = _engine(core, helpers + near, topo)
    g.wait_ge(S.ld, 32)
    _send(g, T, topo, helpers, s, eng, S.hop)
    _send(g, T, topo, near, s, eng, S.near)

    for q, r0, c0 in ((g.sync, 0, 0), (g.scalar, hr, D)):
        q.wait_ge(S.ld, 32)
        q.wait_ge(S.near, len(near))
        q.dma_start(T.uv[R * a0:R * a1, c0:c0 + D], T.gat[a0:a1, r0:r0 + hr, :]).then_inc(S.gnear, 16)
        q.wait_ge(S.far, len(other))
        q.dma_start(T.uv[R * b0:R * b1, c0:c0 + D], T.gat[b0:b1, r0:r0 + hr, :]).then_inc(S.gfar, 16)

    K = N * R
    g.tensor.wait_ge(S.gnear, 32)
    g.tensor.wait_ge(S.gfar, 32)
    g.tensor.matmul(T.wp[:, 0:D], T.uv[0:K, 0:D], T.uv[0:K, D:2 * D], True, True).then_inc(S.mw, 1)
    g.vector.wait_ge(S.mw, 1)
    g.vector.tensor_copy(T.wb[:, :], T.wp[:, 0:D]).then_inc(S.cw, 1)
    g.tensor.wait_ge(S.xl, 16)
    g.tensor.wait_ge(S.cw, 1)
    g.tensor.matmul(T.yp0[:, 0:HALF], T.wb[:, :], T.xs[:, 0:HALF], True, True).then_inc(S.my0, 1)
    g.tensor.matmul(T.yp1[:, 0:HALF], T.wb[:, :], T.xs[:, HALF:TK], True, True).then_inc(S.my1, 1)
    g.vector.wait_ge(S.my0, 1)
    g.vector.tensor_copy(T.ys[:, 0:HALF], T.yp0[:, 0:HALF]).then_inc(S.cy0, 1)
    g.vector.wait_ge(S.my1, 1)
    g.vector.tensor_copy(T.ys[:, HALF:TK], T.yp1[:, 0:HALF]).then_inc(S.cy1, 1)
    g.sync.wait_ge(S.cy0, 1)
    g.sync.dma_start(T.y[:, 0:HALF], T.ys[:, 0:HALF]).then_inc(S.st, 16)
    g.scalar.wait_ge(S.cy1, 1)
    g.scalar.dma_start(T.y[:, HALF:TK], T.ys[:, HALF:TK]).then_inc(S.st, 16)

    g.wait_ge(S.sent, 2)
    g.wait_ge(S.st, 32)
